import numpy as np, ml_dtypes
CORES = [9,10,11,14,17,18,19,22,49,50,51,54]
N = 12
import mx_ref
NC = 256
CNT = [[0,120,0,0,0,0,48,32,56,0,0,0],[32,0,0,96,0,48,0,0,0,80,0,0],[40,8,112,64,0,16,0,0,0,0,0,16],[120,0,0,0,0,72,0,0,0,64,0,0],[0,32,80,0,0,40,0,56,32,16,0,0],[0,0,48,0,120,0,56,0,0,0,32,0],[16,56,0,0,48,0,0,32,40,0,0,64],[0,0,0,32,0,0,112,56,0,0,0,56],[0,0,0,0,40,0,0,24,88,0,72,32],[0,0,0,80,0,24,0,0,72,0,0,80],[0,0,0,0,120,24,32,8,0,0,0,72],[0,0,0,0,72,0,0,64,0,0,48,72]]
OFF = [[sum(c[:e]) for e in range(N + 1)] for c in CNT]
TOT = [sum(c[e] for c in CNT) for e in range(N)]
BF = ml_dtypes.bfloat16
def setup_inputs(rng):
    def f(*shape):
        return mx_ref.flush((rng.standard_normal(shape, dtype=np.float32) * np.exp2(rng.integers(-2, 3, shape[:-1] + (1,)))).astype(BF))
    return {"w": f(N, 128, 512), "x": f(N, 128, 4 * NC)}
def setup_inputs_blocks(rng):
    d = setup_inputs(rng)
    for k in ("w", "x"): d[k] = mx_ref.spread(d[k], rng, 4)
    return d
def setup_inputs_wide(rng):
    d = setup_inputs(rng)
    for k in ("w", "x"): d[k] = mx_ref.flush((d[k].astype(np.float32) * np.exp2(rng.integers(-10, 11, (N, 1, 1))).astype(np.float32)).astype(BF))
    return d
def setup_inputs_zeros(rng):
    d = setup_inputs(rng); v = d["x"].reshape(N, 128, -1, 4).copy()
    v[np.broadcast_to((rng.random((N, 1, v.shape[2], 1)) < 0.33), v.shape)] = 0
    d["x"] = v.reshape(d["x"].shape)
    return d
def reference(w, x):
    y = np.full((N, 128, max(TOT)), np.nan, np.float32)
    for e in range(N):
        t = np.concatenate([x[j][:, 4 * OFF[j][e]:4 * OFF[j][e + 1]] for j in range(N)], axis=1)
        y[e][:, :TOT[e]] = mx_ref.matmul(mx_ref.quantize(w[e]), mx_ref.quantize(t))
    return {"y": y}

from concourse.bass import DstId, RemoteDMATransfer
from concourse.mybir import dt, ActivationFunctionType

NCOL = 256
MINW = 128
BANK = 512
CALL_COST = 48
NBANK = 8

SCRATCH = {
    "xs": ("sbuf", [128, 4 * NCOL], "bfloat16"),
    "ws": ("sbuf", [128, 512], "bfloat16"),
    "wq": ("sbuf", [128, 128], "float8_e4m3fn_x4"),
    "wp": ("sbuf", [128, 128], "uint8"),
    "q0": ("sbuf", [128, NCOL], "float8_e4m3fn_x4"),
    "p0": ("sbuf", [128, NCOL], "uint8"),
    "q1": ("sbuf", [128, NCOL], "float8_e4m3fn_x4"),
    "p1": ("sbuf", [128, NCOL], "uint8"),
    "rq": ("sbuf", [128, NCOL], "float8_e4m3fn_x4"),
    "rp": ("sbuf", [128, NCOL], "uint8"),
    "lq": ("sbuf", [128, 1024], "float8_e4m3fn_x4"),
    "lp": ("sbuf", [128, 1024], "uint8"),
    "ps": ("psum", [128, BANK * NBANK], "float32"),
    "ysb": ("sbuf", [128, 512], "float32"),
}
SEMAPHORES = (["ld0", "ld1", "ldw", "qx0", "qx1", "qw", "rlc", "rls", "sent", "stA", "stB"]
              + ["arr%d" % i for i in range(3)] + ["mm%d" % i for i in range(NBANK)] + ["cp%d" % i for i in range(4)])


def _bits(m):
    return [i for i in range(16) if (m >> i) & 1]


def _deal(pool, weights):
    m, size = len(weights), 1
    while size * 2 * m <= len(pool):
        size *= 2
    sizes = [size] * m
    left = len(pool) - size * m
    for i in sorted(range(m), key=lambda i: -weights[i]):
        if left >= sizes[i]:
            left -= sizes[i]
            sizes[i] *= 2
    out, k = [], 0
    for s in sizes:
        out.append(pool[k:k + s])
        k += s
    return out


def _classes(runs):
    rs = sorted(runs, key=lambda r: -r["c"])
    n = len(rs)
    best, cut = [0] + [None] * n, [0] * (n + 1)
    for i in range(1, n + 1):
        for k in range(i):
            v = best[k] + CALL_COST + rs[k]["c"] * (i - k)
            if best[i] is None or v < best[i]:
                best[i], cut[i] = v, k
    out, i = [], n
    while i > 0:
        out.append(rs[cut[i]:i])
        i = cut[i]
    return out[::-1]


def make_plan(cores, CNT, topo):
    N = len(cores)
    OFF = [[sum(r[:e]) for e in range(N + 1)] for r in CNT]
    chip = [topo.chip(c) for c in cores]
    runs = [[{"j": j, "e": e, "a": OFF[j][e], "c": CNT[j][e]} for e in range(N) if CNT[j][e] and e != j] for j in range(N)]
    for j in range(N):
        for r in runs[j]:
            r["off"] = chip[j] != chip[r["e"]]
            r["relay"] = not topo.may_write(cores[j], cores[r["e"]])
    noff = [sum(1 for r in runs[j] if r["off"] and not r["relay"]) for j in range(N)]
    core = {c: {"calls": [[], [], []], "relay": False} for c in cores}
    deliv = []

    for j in range(N):
        s = min((OFF[j][e] for e in range(1, N)), key=lambda v: (abs(v - NCOL // 2), v))
        wins = [(0, max(s, MINW)), (min(s, MINW), NCOL)]
        score = []
        for part in (0, 1):
            mine = [r for r in runs[j] if (r["a"] >= s) == (part == 1)]
            score.append((sum(1 for r in mine if r["relay"]), sum(1 for r in mine if r["off"])))
        first = 1 if score[1] > score[0] else 0
        order = [first, 1 - first]
        w0 = wins[first]
        rest = (w0[1], NCOL) if first == 0 else (0, w0[0])
        P = core[cores[j]]
        P["pieces"] = [wins[order[0]], wins[order[1]]]
        P["loads"] = [w0, rest]
        for r in runs[j]:
            r["ph"] = order.index(1 if r["a"] >= s else 0)
        P["own"] = None
        if CNT[j][j]:
            ph = order.index(1 if OFF[j][j] >= s else 0)
            wa, wb = P["pieces"][ph]
            st = min(OFF[j][j] - wa, wb - wa - MINW)
            P["own"] = {"ph": ph, "lo": st, "n": MINW, "u": OFF[j][j] - wa - st, "c": CNT[j][j]}

    def window(a, c, W, lo, hi):
        st = max(lo, min(a, hi - W))
        return st, a - st

    for j in range(N):
        rel = [r for r in runs[j] if r["relay"]]
        if not rel:
            continue
        src = cores[j]
        ph = rel[0]["ph"]
        wa, wb = core[src]["pieces"][ph]
        cands = [k for k in range(N) if k != j and chip[k] == chip[j]
                 and all(topo.may_write(cores[k], cores[r["e"]]) for r in rel)]
        cands.sort(key=lambda k: (noff[k], k))
        jobs = []
        if len(rel) >= 2 and len(cands) >= 2:
            jobs.append((rel[:2], cands[0], cands[1]))
            left, nxt = rel[2:], 2
        else:
            left, nxt = rel, 0
        for r in left:
            k = cands[nxt % len(cands)]
            jobs.append(([r], k, k))
            nxt += 1
        W1 = max(g[-1]["a"] + g[-1]["c"] - g[0]["a"] for g, _, _ in jobs)
        hop1 = {"c": [], "s": []}
        for g, kc, ks in jobs:
            st, _ = window(g[0]["a"], g[-1]["a"] + g[-1]["c"] - g[0]["a"], W1, wa, wb)
            W2 = max(r["c"] for r in g)
            ds = []
            for r in g:
                st2, u = window(r["a"] - st, r["c"], W2, 0, W1)
                d = {"j": j, "e": r["e"], "c": r["c"], "W": W2, "u": u, "stage": 2, "scol": st2}
                deliv.append(d)
                ds.append(d)
            for kind, k, sem in (("c", kc, "rlc"), ("s", ks, "rls")):
                core[cores[k]]["relay"] = True
                it = {"dst": cores[k], "scol": st - wa, "W": W1, "dcol": 0, "sem": sem, "d": None, "c": W1}
                hop1[kind].append(it)
                core[cores[k]]["calls"][2].append({"kind": kind, "bufs": ("rq", "rp"), "crit": True, "wait": (sem, it),
                                                   "items": [{"dst": cores[d["e"]], "scol": d["scol"], "W": W2, "d": d, "c": d["c"]} for d in ds]})
        for kind in ("c", "s"):
            core[src]["calls"][ph].append({"kind": kind, "bufs": ("q%d" % ph, "p%d" % ph), "crit": True, "wait": None, "items": hop1[kind]})

    for j in range(N):
        src = cores[j]
        for ph in (0, 1):
            wa, wb = core[src]["pieces"][ph]
            cl = _classes([r for r in runs[j] if r["ph"] == ph and not r["relay"]])
            cl.sort(key=lambda g: (-sum(1 for r in g if r["off"]), -g[0]["c"]))
            for g in cl:
                W = max(r["c"] for r in g)
                items = []
                for r in g:
                    st, u = window(r["a"], r["c"], W, wa, wb)
                    d = {"j": j, "e": r["e"], "c": r["c"], "W": W, "u": u, "stage": 1 if r["off"] else 0}
                    deliv.append(d)
                    items.append({"dst": cores[r["e"]], "scol": st - wa, "W": W, "d": d, "c": r["c"]})
                for kind in ("c", "s"):
                    core[src]["calls"][ph].append({"kind": kind, "bufs": ("q%d" % ph, "p%d" % ph), "crit": False, "wait": None,
                                                   "items": [dict(it) for it in items]})

    for e in range(N):
        P = core[cores[e]]
        ds = [d for d in deliv if d["e"] == e]
        pos, groups, pending = 0, [], []
        for stage in (0, 1, 2):
            pending += sorted((d for d in ds if d["stage"] == stage), key=lambda d: d["j"])
            if pending and pos + sum(d["W"] for d in pending) >= MINW:
                for d in pending:
                    d["pos"], d["grp"] = pos, len(groups)
                    pos += d["W"]
                groups.append(pending)
                pending = []
        assert not pending
        bank = 0
        work = []
        if P["own"]:
            o = P["own"]
            y0 = sum(CNT[k][e] for k in range(e))
            work.append({"own": True, "mm": [(o["lo"], o["n"], bank)], "cp": [(bank * BANK + o["u"], y0, o["c"])], "st": [(y0, y0 + o["c"])]})
            bank += 1
        for gi, g in enumerate(groups):
            chunks, lo = [], g[0]["pos"]
            for d in g:
                if d["pos"] + d["W"] - lo > BANK:
                    chunks.append([lo, d["pos"]])
                    lo = d["pos"]
            chunks.append([lo, g[-1]["pos"] + g[-1]["W"]])
            mm, cp = [], []
            for lo, hi in chunks:
                lo2 = min(lo, hi - MINW)
                assert lo2 >= 0 and hi - lo2 <= BANK
                mm.append((lo2, hi - lo2, bank))
                for d in g:
                    if lo <= d["pos"] < hi:
                        sc = bank * BANK + d["pos"] + d["u"] - lo2
                        y0 = sum(CNT[k][e] for k in range(d["j"]))
                        if cp and cp[-1][0] + cp[-1][2] == sc and cp[-1][1] + cp[-1][2] == y0 and cp[-1][0] // BANK == bank:
                            cp[-1] = (cp[-1][0], cp[-1][1], cp[-1][2] + d["c"])
                        else:
                            cp.append((sc, y0, d["c"]))
                bank += 1
            st = []
            for _, y0, c in sorted(cp, key=lambda t: t[1]):
                if st and st[-1][1] == y0:
                    st[-1] = (st[-1][0], y0 + c)
                else:
                    st.append((y0, y0 + c))
            work.append({"own": False, "grp": gi, "mm": mm, "cp": cp, "st": st})
        assert bank <= NBANK
        P["work"] = work
        P["arr"] = [0] * len(groups)

    for c in cores:
        P = core[c]
        j = cores.index(c)
        others = [d for d in cores if topo.chip(d) != topo.chip(c)]
        offpool = _bits(topo.mask(c, others[0]))
        busy_off = noff[j] > 0 or P["relay"]
        P["sent"] = 0
        for ph in (0, 1, 2):
            for call in P["calls"][ph]:
                on = [it for it in call["items"] if topo.chip(it["dst"]) == topo.chip(c)]
                off = [it for it in call["items"] if topo.chip(it["dst"]) != topo.chip(c)]
                if off:
                    for it, eng in zip(off, _deal(_bits(topo.mask(c, off[0]["dst"])), [it["c"] for it in off])):
                        it["eng"] = eng
                if on:
                    pool = _bits(topo.mask(c, on[0]["dst"]))
                    if off or (busy_off and not call["crit"]):
                        pool = [b for b in pool if b not in offpool]
                    for it, eng in zip(on, _deal(pool, [it["c"] for it in on])):
                        it["eng"] = eng
                for it in call["items"]:
                    P["sent"] += len(it["eng"])
                    if it["d"] is not None:
                        it["dcol"], it["sem"] = it["d"]["pos"], "arr%d" % it["d"]["grp"]
                        it["dbufs"] = ("lq", "lp")
                        core[it["dst"]]["arr"][it["d"]["grp"]] += len(it["eng"])
                    else:
                        it["dbufs"] = ("rq", "rp")
    return core


def rank_program(g, core, T, topo):
    if T.rank_of(core) is None:
        return
    P = make_plan(list(T.cores), T.tables["CNT"], topo)[core]
    S = T.sem

    (a0, b0), (a1, b1) = P["loads"]
    g.sync.dma_start(T.xs[:, 4 * a0:4 * b0], T.x[:, 4 * a0:4 * b0]).then_inc(S.ld0, 16)
    g.scalar.dma_start(T.xs[:, 4 * a1:4 * b1], T.x[:, 4 * a1:4 * b1]).then_inc(S.ld1, 16)
    g.sync.dma_start(T.ws[:], T.w[:]).then_inc(S.ldw, 16)

    for ph in (0, 1):
        wa, wb = P["pieces"][ph]
        g.vector.wait_ge(S["ld%d" % ph], 16)
        g.vector.quantize_mx(T["q%d" % ph][:, 0:wb - wa], T["p%d" % ph][:, 0:wb - wa], T.xs[:, 4 * wa:4 * wb]).then_inc(S["qx%d" % ph], 1)
    g.vector.wait_ge(S.ldw, 16)
    g.vector.quantize_mx(T.wq[:], T.wp[:], T.ws[:]).then_inc(S.qw, 1)

    def view(bufs, kind, a, b):
        return T[bufs[0]][:, a:b].bitcast(dt.uint8) if kind == "c" else T[bufs[1]][:, a:b]

    for ph in (0, 1, 2):
        if ph < 2:
            g.wait_ge(S["qx%d" % ph], 1)
        for call in P["calls"][ph]:
            if call["wait"]:
                g.wait_ge(S[call["wait"][0]], len(call["wait"][1]["eng"]))
            trs = []
            for it in call["items"]:
                rid, pid, _ = topo.addr(it["dst"])
                trs.append(RemoteDMATransfer(dst_ids=[DstId(rid=rid, pnc=pid)], dma_engine_mask=sum(1 << b for b in it["eng"]),
                                             remote_sem=S[it["sem"]],
                                             src=view(call["bufs"], call["kind"], it["scol"], it["scol"] + it["W"]),
                                             dst=view(it["dbufs"], call["kind"], it["dcol"], it["dcol"] + it["W"])))
            g.remote_dma_fused(trs, local_sem=S.sent)
    g.wait_ge(S.sent, P["sent"])

    g.tensor.wait_ge(S.qw, 1)
    nA = nB = 0
    for k, wk in enumerate(P["work"]):
        last = k == len(P["work"]) - 1
        if wk["own"]:
            ph = P["own"]["ph"]
            g.tensor.wait_ge(S["qx%d" % ph], 1)
            cq, cpl = T["q%d" % ph], T["p%d" % ph]
        else:
            g.tensor.wait_ge(S["arr%d" % wk["grp"]], P["arr"][wk["grp"]])
            cq, cpl = T.lq, T.lp
        for lo, n, bank in wk["mm"]:
            g.tensor.matmul_mx(T.ps[:, bank * BANK:bank * BANK + n], T.wq[:], T.wp[:], cq[:, lo:lo + n], cpl[:, lo:lo + n], True, True).then_inc(S["mm%d" % k], 1)
        eng = g.vector if last else g.scalar
        eng.wait_ge(S["mm%d" % k], len(wk["mm"]))
        for sc, y0, c in wk["cp"]:
            if last:
                g.vector.tensor_copy(T.ysb[:, y0:y0 + c], T.ps[:, sc:sc + c]).then_inc(S["cp%d" % k], 1)
            else:
                g.scalar.activation(T.ysb[:, y0:y0 + c], T.ps[:, sc:sc + c], ActivationFunctionType.Copy).then_inc(S["cp%d" % k], 1)
        q = g.sync if last else g.scalar
        q.wait_ge(S["cp%d" % k], len(wk["cp"]))
        for y0, y1 in wk["st"]:
            q.dma_start(T.y[:, y0:y1], T.ysb[:, y0:y1]).then_inc(S.stB if last else S.stA, 16)
            if last:
                nB += 16
            else:
                nA += 16
    if nA:
        g.scalar.wait_ge(S.stA, nA)
    g.sync.wait_ge(S.stB, nB)
